import numpy as np
import ml_dtypes


def mxq(x, axis, fmt="e4m3"):
    dtype, down = {"e4m3": (ml_dtypes.float8_e4m3fn, 7), "e5m2": (ml_dtypes.float8_e5m2, 14)}[fmt]
    v = np.moveaxis(np.asarray(x, np.float32).astype(ml_dtypes.bfloat16).astype(np.float64), axis, -1)
    blocks = v.reshape(v.shape[:-1] + (-1, 32))
    amax = np.abs(blocks).max(-1, keepdims=True)
    byte = np.maximum(np.where(amax > 0, np.frexp(amax)[1] - 1 + 127, 0) - down, 1)
    scale = np.exp2(byte - 127.0)
    codes = (blocks / scale).astype(np.float32).astype(dtype).astype(np.float64)
    return np.moveaxis((codes * scale).reshape(v.shape), -1, axis)


WIDE = False


def mx_kscale(k):
    if not WIDE:
        return np.ones(k)
    levels = np.array([10, -10, 5, -5, 0])
    if k % 512:
        return np.exp2(np.random.permutation(np.resize(levels, k // 32))).repeat(32)
    a = np.empty((k // 512, 16))
    for p in range(k // 512):
        a[p, :8] = np.random.permutation(np.resize(levels, 8))
        for g in range(8):
            far = levels[np.abs(levels - a[p, g]) >= 10]
            a[p, g + 8] = far[np.random.randint(len(far))]
    return np.exp2(a.ravel()).repeat(32)


def f64(x):
    return np.asarray(x).astype(np.float64)


def striped(idx):
    return np.tile(np.asarray(idx).reshape(-1, 16).T, (8, 1)).astype(np.uint16)


def unstriped(offs):
    return offs[:16].T.reshape(-1).astype(np.int64)


E2M1 = np.array([0.0, 0.5, 1.0, 1.5, 2.0, 3.0, 4.0, 6.0, -0.0, -0.5, -1.0, -1.5, -2.0, -3.0, -4.0, -6.0])


def pack_weight(w, fmt):
    k, n = w.shape
    w = f64(np.asarray(w, np.float32).astype(ml_dtypes.bfloat16)).reshape(k // 32, 32, n)
    amax = np.abs(w).max(1)
    if fmt == "e4m3":
        byte = np.frexp(amax)[1] - 1 + 127 - 7
    else:
        mant, ex = np.frexp(amax / 6.0)
        byte = np.where(mant > 0.5, ex, ex - 1) + 127
    byte = np.clip(np.where(amax > 0, byte, 1), 1, 254)
    scaled = (w * np.exp2(127.0 - byte)[:, None, :]).reshape(k, n).astype(np.float32)
    by_word = np.ascontiguousarray(scaled.reshape(k // 512, 128, 4, n).transpose(0, 1, 3, 2))
    if fmt == "e4m3":
        words = by_word.astype(ml_dtypes.float8_e4m3fn).view(np.uint8)
    else:
        c = by_word.astype(ml_dtypes.float4_e2m1fn).view(np.uint8) & 0xF
        words = (c[..., 0::2] | (c[..., 1::2] << 4)).reshape(k // 512, 128, 2 * n)
    return np.ascontiguousarray(words), np.ascontiguousarray(byte.astype(np.uint8).reshape(k // 512, 16, n))


def unpack_weight(words, scales, fmt):
    g, _, n = scales.shape
    words = np.ascontiguousarray(words).reshape(g, 128, n, -1)
    if fmt == "e4m3":
        vals = words.view(ml_dtypes.float8_e4m3fn).astype(np.float64)
    else:
        nib = np.empty((g, 128, n, 4), np.uint8)
        nib[..., 0::2] = words & 0xF
        nib[..., 1::2] = words >> 4
        vals = E2M1[nib]
    vals = vals * np.repeat(np.exp2(scales.astype(np.float64) - 127.0), 8, axis=1)[..., None]
    return vals.transpose(0, 1, 3, 2).reshape(g * 512, n)


def sigmoid(v):
    return 1.0 / (1.0 + np.exp(-v))


def bf(x):
    return np.asarray(x, np.float32).astype(ml_dtypes.bfloat16)


def planes(Y):
    r, m = Y.shape
    b = f64(bf(Y)).reshape(r // 32, 32, m)
    amax = np.abs(b).max(1)
    byte = np.clip(np.where(amax > 0, np.frexp(amax)[1] - 1 + 127 - 7, 1), 1, 254)
    codes = (b * np.exp2(127.0 - byte)[:, None, :]).reshape(r, m).astype(np.float32).astype(ml_dtypes.float8_e4m3fn).view(np.uint8)
    words = codes.reshape(r // 512, 128, 4, m).transpose(0, 1, 3, 2)
    return np.ascontiguousarray(words), np.ascontiguousarray(byte.astype(np.uint8).reshape(r // 512, 16, m))


D, E, T, I, Q, G = 512, 512, 2048, 512, 256, 32


def setup_inputs():
    n = np.random.standard_normal
    idx = np.random.permutation(T)[:I]
    fd = mx_kscale(D)
    fi = mx_kscale(I)
    ti = np.ones(T)
    ti[idx] = fi
    keysp = pack_weight(n((D, T)) / fd[:, None], "e2m1")
    return {
        "query": (n((D, Q)) * 0.8 / np.sqrt(D) * fd[:, None]).astype(np.float32),
        "keys_words": keysp[0],
        "keys_scales": keysp[1],
        "th": (np.random.uniform(-0.5, 0.5, (Q, 1))).astype(np.float32),
        "sharp": (np.random.uniform(1.0, 3.0, (Q, 1))).astype(np.float32),
        "os": (np.random.uniform(0.5, 2.0, (1, I)) * fi).astype(np.float32),
        "vals": (n((E, T)) / ti).astype(np.float32),
        "offs": striped(idx),
    }


def reference(query, keys_words, keys_scales, th, sharp, os, vals, offs):
    idx = unstriped(offs)
    keysu = unpack_weight(keys_words, keys_scales, "e2m1")
    queryq = mxq(f64(query), 0, "e4m3")
    keysidxg = keysu[:, idx]
    a = queryq.T @ keysidxg
    s = a.reshape(Q, G, I // G).mean(axis=2) * f64(sharp)
    p = np.exp(s - np.max(s, axis=1, keepdims=True))
    z = np.sum(p, axis=1, keepdims=True)
    r = p / z
    rr = np.repeat(r, I // G, axis=1)
    w = rr * sigmoid(a - f64(th))
    wo1 = w * f64(os)
    wt1 = wo1.T
    vt1 = f64(vals)[:, idx].T
    vt1q = mxq(vt1, 0, "e4m3")
    wt1q = mxq(wt1, 0, "e4m3")
    o = vt1q.T @ wt1q
    words, scales = planes(o)
    return o, words, scales

@@ -1,0 +1,259 @@
+from contextlib import ExitStack
+
+import concourse.mybir as mybir
+from concourse.masks import make_identity
+
+D, E, T, I, Q, G = 512, 512, 2048, 512, 256, 32
+FLOPS = 2 * D * I * Q + 2 * I * E * Q
+
+F32 = mybir.dt.float32
+BF16 = mybir.dt.bfloat16
+I32 = mybir.dt.int32
+U32 = mybir.dt.uint32
+U16 = mybir.dt.uint16
+U8 = mybir.dt.uint8
+FP8X4 = mybir.dt.float8_e4m3fn_x4
+FP4X4 = mybir.dt.float4_e2m1fn_x4
+ACT = mybir.ActivationFunctionType
+ALU = mybir.AluOpType
+AXIS = mybir.AxisListType
+
+P = 128
+PACK = 4
+HALVES = Q // P
+PAGE = I // G
+RUN = 4
+
+
+def tile_attend_pagetimessigmoid_pl_kernel(tc, query, keys_words, keys_scales, th, sharp, slot_factor, vals, offs, out_0, out_1, out_2):
+    nc = tc.nc
+    with ExitStack() as ctx:
+        sb = ctx.enter_context(tc.tile_pool(name="sb", bufs=1))
+        ps = ctx.enter_context(tc.psum_pool(name="ps", bufs=1))
+
+        offsets = sb.tile([P, I // 16], U16, name="offsets")
+        nc.sync.dma_start(offsets[:], offs)
+
+        key_scale_pool = sb.tile([P, T], U8, name="key_scale_pool", tag="pool_3", align_bytes=64)
+        nc.vector.memset(key_scale_pool[:].bitcast(I32), 0)
+        for quad in range(4):
+            nc.scalar.dma_start(
+                out=key_scale_pool[32 * quad : 32 * quad + 4, :].bitcast(I32),
+                in_=keys_scales[0, 4 * quad : 4 * quad + 4, :].bitcast(I32),
+            )
+        query_rows = sb.tile([P, PACK, Q], F32, name="query_rows", tag="pool_1", align_bytes=64)
+        nc.sync.dma_start(out=query_rows[:], in_=query.rearrange("(p t) q -> p t q", t=PACK))
+        key_word_pool = sb.tile([P, T], U16, name="key_word_pool", tag="pool_2", align_bytes=64)
+        nc.sync.dma_start(out=key_word_pool[:].bitcast(I32), in_=keys_words[0].bitcast(I32))
+
+        identity = sb.tile([P, P], F32, name="identity")
+        make_identity(nc, identity[:])
+        row_terms = sb.tile([P, P], F32, name="row_terms")
+        nc.gpsimd.memset(row_terms[:], 0.0)
+        nc.gpsimd.dma_start(out=row_terms[0:HALVES, :], in_=th.rearrange("(h p) o -> h (p o)", p=P))
+        nc.gpsimd.dma_start(out=row_terms[HALVES : 2 * HALVES, :], in_=sharp.rearrange("(h p) o -> h (p o)", p=P))
+        os_cols = sb.tile([P, PACK], F32, name="os_cols")
+        nc.gpsimd.dma_start(out=os_cols[:], in_=slot_factor.rearrange("o (s r) -> (o s) r", r=PACK))
+
+        value_planes = vals.rearrange("(p t) n -> t p n", t=PACK)
+        value_pools = []
+
+        def load_values(t):
+            pool_t = sb.tile([P, T], F32, name="value_pool_%d" % t, tag="pool_%d" % t, align_bytes=64)
+            nc.sync.dma_start(out=pool_t[:], in_=value_planes[t])
+            value_pools.append(pool_t)
+
+        load_values(0)
+
+        terms_turned = ps.tile([P, P], F32, name="terms_turned")
+        nc.tensor.transpose(terms_turned[:], row_terms[:], identity[:])
+        minus_th = sb.tile([P, HALVES], F32, name="minus_th")
+        nc.vector.tensor_scalar(minus_th[:], terms_turned[:, 0:HALVES], -1.0, None, ALU.mult)
+        minus_sharp = sb.tile([P, HALVES], F32, name="minus_sharp")
+        nc.vector.tensor_scalar(minus_sharp[:], terms_turned[:, HALVES : 2 * HALVES], -1.0 / PAGE, None, ALU.mult)
+
+        key_scales = sb.tile([P, I], U8, name="key_scales", align_bytes=64)
+        nc.vector.tensor_copy(key_scales[:], key_scale_pool[:].indirect(offsets[:]))
+        key_words = sb.tile([P, I], U16, name="key_words", align_bytes=64)
+        nc.vector.tensor_copy(key_words[:], key_word_pool[:].indirect(offsets[:]))
+
+        query_bf = sb.tile([P, Q, PACK], BF16, name="query_bf", align_bytes=64)
+        nc.scalar.copy(
+            out=query_bf[:].rearrange("p (c i) t -> p c t i", i=RUN),
+            in_=query_rows[:].rearrange("p t (c i) -> p c t i", i=RUN),
+        )
+        query_codes = sb.tile([P, Q], U32, name="query_codes", align_bytes=64)
+        query_scales = sb.tile([P, Q], U8, name="query_scales", align_bytes=64)
+        nc.vector.quantize_mx(
+            out=query_codes[:].bitcast(FP8X4), scales=query_scales[:], in_=query_bf[:].rearrange("p q t -> p (q t)")
+        )
+
+        load_values(1)
+        load_values(2)
+        load_values(3)
+
+        halves = [slice(h * P, (h + 1) * P) for h in range(HALVES)]
+        scores = []
+        for h in range(HALVES):
+            bank = ps.tile([P, I], F32, name="scores_%d" % h, tag="half_%d" % h)
+            nc.tensor.matmul_mx(
+                out=bank[:],
+                lhsT=query_codes[:, halves[h]].bitcast(FP8X4),
+                lhsT_scale=query_scales[:, halves[h]],
+                rhs=key_words[:].bitcast(FP4X4),
+                rhs_scale=key_scales[:],
+                start=True,
+                stop=True,
+            )
+            scores.append(bank)
+
+        page_sums = sb.tile([P, HALVES, G], F32, name="page_sums", tag="picked_0", align_bytes=64)
+        minus_s = sb.tile([P, HALVES, G], F32, name="minus_s")
+        minus_top = sb.tile([P, HALVES], F32, name="minus_top")
+        gates = []
+        for h in range(HALVES):
+            nc.vector.tensor_reduce(
+                out=page_sums[:, h, :], in_=scores[h][:].rearrange("p (g j) -> p g j", j=PAGE), axis=AXIS.X, op=ALU.add
+            )
+            gate = sb.tile([P, PACK, P], F32, name="gate_%d" % h)
+            nc.scalar.activation(
+                out=gate[:],
+                in_=scores[h][:].rearrange("p (s r) -> p r s", r=PACK),
+                func=ACT.Sigmoid,
+                bias=minus_th[:, h : h + 1],
+            )
+            gates.append(gate)
+        for h in range(HALVES):
+            nc.vector.tensor_scalar(
+                out=minus_s[:, h, :],
+                in0=page_sums[:, h, :],
+                scalar1=minus_sharp[:, h : h + 1],
+                scalar2=None,
+                op0=ALU.mult,
+                op1=ALU.min,
+                accum_out=minus_top[:, h : h + 1],
+            )
+        sig = sb.tile([P, HALVES, G], F32, name="sig")
+        for h in range(HALVES):
+            nc.scalar.activation(
+                out=sig[:, h, :], in_=minus_s[:, h, :], func=ACT.Sigmoid, scale=-1.0, bias=minus_top[:, h : h + 1]
+            )
+        rest = sb.tile([P, HALVES, G], F32, name="rest")
+        nc.scalar.activation(out=rest[:], in_=sig[:], func=ACT.Copy, scale=-1.0, bias=1.0)
+        rest_inv = sb.tile([P, HALVES, G], F32, name="rest_inv")
+        nc.vector.reciprocal(out=rest_inv[:], in_=rest[:])
+        page_exp = sb.tile([P, HALVES, G], F32, name="page_exp")
+        row_sum = sb.tile([P, HALVES], F32, name="row_sum", tag="picked_1", align_bytes=64)
+        for h in range(HALVES):
+            nc.vector.scalar_tensor_tensor(
+                out=page_exp[:, h, :],
+                in0=sig[:, h, :],
+                scalar=1.0,
+                in1=rest_inv[:, h, :],
+                op0=ALU.mult,
+                op1=ALU.mult,
+                accum_out=row_sum[:, h : h + 1],
+            )
+        row_inv = sb.tile([P, HALVES], F32, name="row_inv")
+        nc.vector.reciprocal(out=row_inv[:], in_=row_sum[:])
+        shares = sb.tile([P, HALVES, P], F32, name="shares")
+        shares_turned = ps.tile([P, Q], F32, name="shares_turned")
+        for h in range(HALVES):
+            nc.scalar.activation(
+                out=shares[:, h, :].rearrange("p (g j) -> p g j", j=P // G),
+                in_=page_exp[:, h, :].rearrange("p (g o) -> p g o", o=1).to_broadcast([P, G, P // G]),
+                func=ACT.Copy,
+                scale=row_inv[:, h : h + 1],
+            )
+            nc.tensor.transpose(shares_turned[:, halves[h]], shares[:, h, :], identity[:])
+
+        gated = sb.tile([P, PACK, Q], F32, name="gated", tag="picked_2", align_bytes=64)
+        for pair in range(PACK // 2):
+            turned = ps.tile([P, 2, Q], F32, name="gates_turned_%d" % pair)
+            for h in range(HALVES):
+                for e in range(2):
+                    nc.tensor.transpose(turned[:, e, halves[h]], gates[h][:, 2 * pair + e, :], identity[:])
+            for e in range(2):
+                r = 2 * pair + e
+                nc.scalar.activation(out=gated[:, r, :], in_=turned[:, e, :], func=ACT.Copy, scale=os_cols[:, r : r + 1])
+
+        weight_codes, weight_scales = [], []
+        weights_bf = []
+        for h in range(HALVES):
+            w_bf = sb.tile([P, P, PACK], BF16, name="weights_bf_%d" % h, align_bytes=64)
+            nc.vector.tensor_tensor(
+                out=w_bf[:].rearrange("p (c i) r -> p c r i", i=RUN),
+                in0=gated[:, :, halves[h]].rearrange("p r (c i) -> p c r i", i=RUN),
+                in1=shares_turned[:, halves[h]]
+                .rearrange("p (c o i) -> p c o i", o=1, i=RUN)
+                .to_broadcast([P, P // RUN, PACK, RUN]),
+                op=ALU.mult,
+            )
+            weights_bf.append(w_bf)
+        for h in range(HALVES):
+            codes = sb.tile([P, P], U32, name="weight_codes_%d" % h, align_bytes=64)
+            scales = sb.tile([P, P], U8, name="weight_scales_%d" % h, align_bytes=64)
+            nc.vector.quantize_mx(
+                out=codes[:].bitcast(FP8X4), scales=scales[:], in_=weights_bf[h][:].rearrange("p q r -> p (q r)")
+            )
+            weight_codes.append(codes)
+            weight_scales.append(scales)
+
+        results = [ps.tile([P, PACK, P], F32, name="result_%d" % h, tag="half_%d" % h) for h in range(HALVES)]
+        out_planes = out_0.rearrange("(p t) q -> t p q", t=PACK)
+
+        def store_plane(t):
+            plane = sb.tile([P, Q], F32, name="out_plane_%d" % t)
+            for h in range(HALVES):
+                nc.scalar.copy(out=plane[:, halves[h]], in_=results[h][:, t, :])
+            return plane
+
+        for t in range(PACK):
+            picked = sb.tile([P, I], BF16, name="picked_%d" % t, tag="picked_%d" % t, align_bytes=64)
+            nc.vector.tensor_copy(picked[:], value_pools[t][:].indirect(offsets[:]))
+            pairs = picked[:].bitcast(F32)
+            turned = ps.tile([P, 2, P], F32, name="values_turned_%d" % t, tag="values_turned_%d" % (t % 2))
+            for u in range(2):
+                nc.tensor.transpose(turned[:, u, :], pairs[:, u::2], identity[:])
+            v_bf = sb.tile([P, P, PACK], BF16, name="values_bf_%d" % t, align_bytes=64)
+            nc.scalar.copy(
+                out=v_bf[:].rearrange("p e r -> p (e r)").bitcast(F32).rearrange("p (e u) -> p e u", u=2),
+                in_=turned[:].rearrange("p u e -> p e u"),
+            )
+            v_codes = sb.tile([P, P], U32, name="value_codes_%d" % t, align_bytes=64)
+            v_scales = sb.tile([P, P], U8, name="value_scales_%d" % t, align_bytes=64)
+            nc.vector.quantize_mx(
+                out=v_codes[:].bitcast(FP8X4), scales=v_scales[:], in_=v_bf[:].rearrange("p e r -> p (e r)")
+            )
+            for h in range(HALVES):
+                nc.tensor.matmul_mx(
+                    out=results[h][:, t, :],
+                    lhsT=v_codes[:].bitcast(FP8X4),
+                    lhsT_scale=v_scales[:],
+                    rhs=weight_codes[h][:].bitcast(FP8X4),
+                    rhs_scale=weight_scales[h][:],
+                    start=True,
+                    stop=True,
+                )
+            if t < PACK - 1:
+                nc.sync.dma_start(out=out_planes[t], in_=store_plane(t)[:])
+
+        out_bf = [sb.tile([P, P, PACK], BF16, name="out_bf_%d" % h, align_bytes=64) for h in range(HALVES)]
+        nc.vector.tensor_copy(out=out_bf[0][:], in_=results[0][:].rearrange("p t q -> p q t"))
+        nc.scalar.copy(out=out_bf[1][:], in_=results[1][:].rearrange("p t q -> p q t"))
+        out_codes = sb.tile([P, Q], U32, name="out_codes", align_bytes=64)
+        out_scales = sb.tile([P, Q], U8, name="out_scales", align_bytes=64)
+        for h in range(HALVES):
+            nc.vector.quantize_mx(
+                out=out_codes[:, halves[h]].bitcast(FP8X4),
+                scales=out_scales[:, halves[h]],
+                in_=out_bf[h][:].rearrange("p q t -> p (q t)"),
+            )
+        nc.scalar.dma_start(out=out_planes[PACK - 1], in_=store_plane(PACK - 1)[:])
+        nc.sync.dma_start(out=out_1[0].rearrange("p c r -> p (c r)").bitcast(I32), in_=out_codes[:].bitcast(I32))
+        for quad in range(4):
+            queue = nc.sync if quad < 2 else nc.scalar
+            queue.dma_start(
+                out=out_2[0, 4 * quad : 4 * quad + 4, :].bitcast(I32),
+                in_=out_scales[32 * quad : 32 * quad + 4, :].bitcast(I32),
+            )

@@ -29,68 +29,81 @@ def tile_attend_pagetimessigmoid_pl_kernel(tc, query, keys_words, keys_scales, t
     nc = tc.nc
     with ExitStack() as ctx:
         sb = ctx.enter_context(tc.tile_pool(name="sb", bufs=1))
+        lane = ctx.enter_context(tc.tile_pool(name="lane", bufs=1))
         ps = ctx.enter_context(tc.psum_pool(name="ps", bufs=1))
 
         offsets = sb.tile([P, I // 16], U16, name="offsets")
         nc.sync.dma_start(offsets[:], offs)
 
-        key_scale_pool = sb.tile([P, T], U8, name="key_scale_pool", tag="pool_3", align_bytes=64)
+        key_word_pool = sb.tile([P, T], U16, name="key_word_pool", tag="pool_2", align_bytes=64)
+        nc.sync.dma_start(out=key_word_pool[:].bitcast(I32), in_=keys_words[0].bitcast(I32))
+        query_rows = sb.tile([P, PACK, Q], F32, name="query_rows")
+        nc.sync.dma_start(out=query_rows[:], in_=query.rearrange("(p t) q -> p t q", t=PACK))
+
+        warm_in = sb.tile([P, 1], F32, name="warm_in", tag="pool_0", align_bytes=64)
+        warm_out = sb.tile([P, 1], F32, name="warm_out", tag="pool_1", align_bytes=64)
+        nc.vector.memset(warm_in[:], 0.0)
+        nc.scalar.activation(out=warm_out[:], in_=warm_in[:], func=ACT.Sigmoid)
+
+        key_scale_pool = lane.tile([P, T], U8, name="key_scale_pool", offset=0, align_bytes=64)
         nc.vector.memset(key_scale_pool[:].bitcast(I32), 0)
         for quad in range(4):
-            nc.scalar.dma_start(
+            nc.sync.dma_start(
                 out=key_scale_pool[32 * quad : 32 * quad + 4, :].bitcast(I32),
                 in_=keys_scales[0, 4 * quad : 4 * quad + 4, :].bitcast(I32),
             )
-        query_rows = sb.tile([P, PACK, Q], F32, name="query_rows", tag="pool_1", align_bytes=64)
-        nc.sync.dma_start(out=query_rows[:], in_=query.rearrange("(p t) q -> p t q", t=PACK))
-        key_word_pool = sb.tile([P, T], U16, name="key_word_pool", tag="pool_2", align_bytes=64)
-        nc.sync.dma_start(out=key_word_pool[:].bitcast(I32), in_=keys_words[0].bitcast(I32))
 
-        identity = sb.tile([P, P], F32, name="identity")
-        make_identity(nc, identity[:])
         row_terms = sb.tile([P, P], F32, name="row_terms")
         nc.gpsimd.memset(row_terms[:], 0.0)
-        nc.gpsimd.dma_start(out=row_terms[0:HALVES, :], in_=th.rearrange("(h p) o -> h (p o)", p=P))
         nc.gpsimd.dma_start(out=row_terms[HALVES : 2 * HALVES, :], in_=sharp.rearrange("(h p) o -> h (p o)", p=P))
+        nc.gpsimd.dma_start(out=row_terms[0:HALVES, :], in_=th.rearrange("(h p) o -> h (p o)", p=P))
+        identity = sb.tile([P, P], F32, name="identity")
+        make_identity(nc, identity[:])
         os_cols = sb.tile([P, PACK], F32, name="os_cols")
         nc.gpsimd.dma_start(out=os_cols[:], in_=slot_factor.rearrange("o (s r) -> (o s) r", r=PACK))
 
         value_planes = vals.rearrange("(p t) n -> t p n", t=PACK)
         value_pools = []
 
-        def load_values(t):
-            pool_t = sb.tile([P, T], F32, name="value_pool_%d" % t, tag="pool_%d" % t, align_bytes=64)
-            nc.sync.dma_start(out=pool_t[:], in_=value_planes[t])
+        def load_values(t, pieces=1):
+            if t == PACK - 1:
+                pool_t = lane.tile([P, T], F32, name="value_pool_%d" % t, offset=0, align_bytes=64)
+            else:
+                pool_t = sb.tile([P, T], F32, name="value_pool_%d" % t, tag="pool_%d" % t, align_bytes=64)
+            for j in range(pieces):
+                cols = slice(j * T // pieces, (j + 1) * T // pieces)
+                nc.sync.dma_start(out=pool_t[:, cols], in_=value_planes[t][:, cols])
             value_pools.append(pool_t)
 
         load_values(0)
+        load_values(1)
 
-        terms_turned = ps.tile([P, P], F32, name="terms_turned")
+        terms_turned = ps.tile([P, P], F32, name="terms_turned", tag="half_0")
         nc.tensor.transpose(terms_turned[:], row_terms[:], identity[:])
         minus_th = sb.tile([P, HALVES], F32, name="minus_th")
-        nc.vector.tensor_scalar(minus_th[:], terms_turned[:, 0:HALVES], -1.0, None, ALU.mult)
+        nc.scalar.activation(out=minus_th[:], in_=terms_turned[:, 0:HALVES], func=ACT.Copy, scale=-1.0)
         minus_sharp = sb.tile([P, HALVES], F32, name="minus_sharp")
-        nc.vector.tensor_scalar(minus_sharp[:], terms_turned[:, HALVES : 2 * HALVES], -1.0 / PAGE, None, ALU.mult)
+        nc.scalar.activation(
+            out=minus_sharp[:], in_=terms_turned[:, HALVES : 2 * HALVES], func=ACT.Copy, scale=-1.0 / PAGE
+        )
 
-        key_scales = sb.tile([P, I], U8, name="key_scales", align_bytes=64)
-        nc.vector.tensor_copy(key_scales[:], key_scale_pool[:].indirect(offsets[:]))
         key_words = sb.tile([P, I], U16, name="key_words", align_bytes=64)
         nc.vector.tensor_copy(key_words[:], key_word_pool[:].indirect(offsets[:]))
+        key_scales = sb.tile([P, I], U8, name="key_scales", align_bytes=64)
+        nc.vector.tensor_copy(key_scales[:], key_scale_pool[:].indirect(offsets[:]))
 
         query_bf = sb.tile([P, Q, PACK], BF16, name="query_bf", align_bytes=64)
         nc.scalar.copy(
             out=query_bf[:].rearrange("p (c i) t -> p c t i", i=RUN),
             in_=query_rows[:].rearrange("p t (c i) -> p c t i", i=RUN),
         )
-        query_codes = sb.tile([P, Q], U32, name="query_codes", align_bytes=64)
+        query_codes = lane.tile([P, Q], U32, name="query_codes", offset=0, align_bytes=64)
         query_scales = sb.tile([P, Q], U8, name="query_scales", align_bytes=64)
         nc.vector.quantize_mx(
             out=query_codes[:].bitcast(FP8X4), scales=query_scales[:], in_=query_bf[:].rearrange("p q t -> p (q t)")
         )
 
-        load_values(1)
-        load_values(2)
-        load_values(3)
+        load_values(2, pieces=2)
 
         halves = [slice(h * P, (h + 1) * P) for h in range(HALVES)]
         scores = []
@@ -107,14 +120,16 @@ def tile_attend_pagetimessigmoid_pl_kernel(tc, query, keys_words, keys_scales, t
             )
             scores.append(bank)
 
-        page_sums = sb.tile([P, HALVES, G], F32, name="page_sums", tag="picked_0", align_bytes=64)
-        minus_s = sb.tile([P, HALVES, G], F32, name="minus_s")
+        load_values(3)
+
+        picked_0 = sb.tile([P, I], BF16, name="picked_0", align_bytes=64)
+        nc.vector.tensor_copy(picked_0[:], value_pools[0][:].indirect(offsets[:]))
+
+        page_sums = sb.tile([P, HALVES, G], F32, name="page_sums", tag="pool_0", align_bytes=64)
+        minus_s = sb.tile([P, HALVES, G], F32, name="minus_s", tag="gated", align_bytes=64)
         minus_top = sb.tile([P, HALVES], F32, name="minus_top")
         gates = []
         for h in range(HALVES):
-            nc.vector.tensor_reduce(
-                out=page_sums[:, h, :], in_=scores[h][:].rearrange("p (g j) -> p g j", j=PAGE), axis=AXIS.X, op=ALU.add
-            )
             gate = sb.tile([P, PACK, P], F32, name="gate_%d" % h)
             nc.scalar.activation(
                 out=gate[:],
@@ -123,6 +138,10 @@ def tile_attend_pagetimessigmoid_pl_kernel(tc, query, keys_words, keys_scales, t
                 bias=minus_th[:, h : h + 1],
             )
             gates.append(gate)
+        for h in range(HALVES):
+            nc.vector.tensor_reduce(
+                out=page_sums[:, h, :], in_=scores[h][:].rearrange("p (g j) -> p g j", j=PAGE), axis=AXIS.X, op=ALU.add
+            )
         for h in range(HALVES):
             nc.vector.tensor_scalar(
                 out=minus_s[:, h, :],
@@ -142,8 +161,8 @@ def tile_attend_pagetimessigmoid_pl_kernel(tc, query, keys_words, keys_scales, t
         nc.scalar.activation(out=rest[:], in_=sig[:], func=ACT.Copy, scale=-1.0, bias=1.0)
         rest_inv = sb.tile([P, HALVES, G], F32, name="rest_inv")
         nc.vector.reciprocal(out=rest_inv[:], in_=rest[:])
-        page_exp = sb.tile([P, HALVES, G], F32, name="page_exp")
-        row_sum = sb.tile([P, HALVES], F32, name="row_sum", tag="picked_1", align_bytes=64)
+        page_exp = sb.tile([P, HALVES, G], F32, name="page_exp", tag="pool_bf", align_bytes=64)
+        row_sum = sb.tile([P, HALVES], F32, name="row_sum", tag="values_bf_1", align_bytes=64)
         for h in range(HALVES):
             nc.vector.scalar_tensor_tensor(
                 out=page_exp[:, h, :],
@@ -157,7 +176,7 @@ def tile_attend_pagetimessigmoid_pl_kernel(tc, query, keys_words, keys_scales, t
         row_inv = sb.tile([P, HALVES], F32, name="row_inv")
         nc.vector.reciprocal(out=row_inv[:], in_=row_sum[:])
         shares = sb.tile([P, HALVES, P], F32, name="shares")
-        shares_turned = ps.tile([P, Q], F32, name="shares_turned")
+        shares_turned = ps.tile([P, Q], F32, name="shares_turned", tag="shares_turned")
         for h in range(HALVES):
             nc.scalar.activation(
                 out=shares[:, h, :].rearrange("p (g j) -> p g j", j=P // G),
@@ -167,23 +186,28 @@ def tile_attend_pagetimessigmoid_pl_kernel(tc, query, keys_words, keys_scales, t
             )
             nc.tensor.transpose(shares_turned[:, halves[h]], shares[:, h, :], identity[:])
 
-        gated = sb.tile([P, PACK, Q], F32, name="gated", tag="picked_2", align_bytes=64)
+        gated = sb.tile([P, Q // RUN, PACK, RUN], F32, name="gated", tag="gated", align_bytes=64)
         for pair in range(PACK // 2):
-            turned = ps.tile([P, 2, Q], F32, name="gates_turned_%d" % pair)
+            turned = ps.tile([P, 2, Q], F32, name="gates_turned_%d" % pair, tag="gates_turned_%d" % pair)
             for h in range(HALVES):
                 for e in range(2):
                     nc.tensor.transpose(turned[:, e, halves[h]], gates[h][:, 2 * pair + e, :], identity[:])
             for e in range(2):
                 r = 2 * pair + e
-                nc.scalar.activation(out=gated[:, r, :], in_=turned[:, e, :], func=ACT.Copy, scale=os_cols[:, r : r + 1])
+                nc.scalar.activation(
+                    out=gated[:, :, r, :],
+                    in_=turned[:, e, :].rearrange("p (c i) -> p c i", i=RUN),
+                    func=ACT.Copy,
+                    scale=os_cols[:, r : r + 1],
+                )
 
         weight_codes, weight_scales = [], []
         weights_bf = []
         for h in range(HALVES):
-            w_bf = sb.tile([P, P, PACK], BF16, name="weights_bf_%d" % h, align_bytes=64)
+            w_bf = sb.tile([P, P, PACK], BF16, name="weights_bf_%d" % h, tag="weights_bf_%d" % h, align_bytes=64)
             nc.vector.tensor_tensor(
                 out=w_bf[:].rearrange("p (c i) r -> p c r i", i=RUN),
-                in0=gated[:, :, halves[h]].rearrange("p r (c i) -> p c r i", i=RUN),
+                in0=gated[:, h * P // RUN : (h + 1) * P // RUN, :, :],
                 in1=shares_turned[:, halves[h]]
                 .rearrange("p (c o i) -> p c o i", o=1, i=RUN)
                 .to_broadcast([P, P // RUN, PACK, RUN]),
@@ -200,43 +224,69 @@ def tile_attend_pagetimessigmoid_pl_kernel(tc, query, keys_words, keys_scales, t
             weight_scales.append(scales)
 
         results = [ps.tile([P, PACK, P], F32, name="result_%d" % h, tag="half_%d" % h) for h in range(HALVES)]
-        out_planes = out_0.rearrange("(p t) q -> t p q", t=PACK)
+        out_rows = out_0.rearrange("(p t) q -> p t q", t=PACK)
 
-        def store_plane(t):
-            plane = sb.tile([P, Q], F32, name="out_plane_%d" % t)
-            for h in range(HALVES):
-                nc.scalar.copy(out=plane[:, halves[h]], in_=results[h][:, t, :])
-            return plane
-
-        for t in range(PACK):
-            picked = sb.tile([P, I], BF16, name="picked_%d" % t, tag="picked_%d" % t, align_bytes=64)
+        def pick(t, tag):
+            picked = sb.tile([P, I], BF16, name="picked_%d" % t, tag=tag, align_bytes=64)
             nc.vector.tensor_copy(picked[:], value_pools[t][:].indirect(offsets[:]))
-            pairs = picked[:].bitcast(F32)
-            turned = ps.tile([P, 2, P], F32, name="values_turned_%d" % t, tag="values_turned_%d" % (t % 2))
-            for u in range(2):
-                nc.tensor.transpose(turned[:, u, :], pairs[:, u::2], identity[:])
-            v_bf = sb.tile([P, P, PACK], BF16, name="values_bf_%d" % t, align_bytes=64)
-            nc.scalar.copy(
-                out=v_bf[:].rearrange("p e r -> p (e r)").bitcast(F32).rearrange("p (e u) -> p e u", u=2),
-                in_=turned[:].rearrange("p u e -> p e u"),
+            return picked
+
+        def pick_on_scalar(t, pieces):
+            pool_bf = sb.tile([P, T], BF16, name="value_pool_bf", tag="pool_bf", align_bytes=64)
+            for j in range(pieces):
+                cols = slice(j * T // pieces, (j + 1) * T // pieces)
+                nc.scalar.activation(out=pool_bf[:, cols], in_=value_pools[t][:, cols], func=ACT.Copy)
+            picked = sb.tile([P, I], BF16, name="picked_%d" % t, tag="weights_bf_0", align_bytes=64)
+            nc.scalar.activation(out=picked[:], in_=pool_bf[:].indirect(offsets[:]), func=ACT.Copy)
+            return picked
+
+        def turn(first, picks, bank_tag, copy):
+            n = len(picks)
+            turned = ps.tile([P, n, 2, P], F32, name="values_turned_%d" % first, tag=bank_tag)
+            for j in range(n):
+                pairs = picks[j][:].bitcast(F32)
+                for u in range(2):
+                    nc.tensor.transpose(turned[:, j, u, :], pairs[:, u::2], identity[:])
+            v_bf = sb.tile([P, n * P * PACK], BF16, name="values_bf_%d" % first, tag="values_bf_%d" % first, align_bytes=64)
+            copy(
+                out=v_bf[:].bitcast(F32).rearrange("p (j e u) -> p j e u", j=n, u=2),
+                in_=turned[:].rearrange("p j u e -> p j e u"),
             )
-            v_codes = sb.tile([P, P], U32, name="value_codes_%d" % t, align_bytes=64)
-            v_scales = sb.tile([P, P], U8, name="value_scales_%d" % t, align_bytes=64)
-            nc.vector.quantize_mx(
-                out=v_codes[:].bitcast(FP8X4), scales=v_scales[:], in_=v_bf[:].rearrange("p e r -> p (e r)")
-            )
-            for h in range(HALVES):
-                nc.tensor.matmul_mx(
-                    out=results[h][:, t, :],
-                    lhsT=v_codes[:].bitcast(FP8X4),
-                    lhsT_scale=v_scales[:],
-                    rhs=weight_codes[h][:].bitcast(FP8X4),
-                    rhs_scale=weight_scales[h][:],
-                    start=True,
-                    stop=True,
-                )
-            if t < PACK - 1:
-                nc.sync.dma_start(out=out_planes[t], in_=store_plane(t)[:])
+            return v_bf
+
+        def multiply(first, n, v_bf, v_codes):
+            v_scales = sb.tile([P, n * P], U8, name="value_scales_%d" % first, align_bytes=64)
+            nc.vector.quantize_mx(out=v_codes[:].bitcast(FP8X4), scales=v_scales[:], in_=v_bf[:])
+            for j in range(n):
+                cols = slice(j * P, (j + 1) * P)
+                for h in range(HALVES):
+                    nc.tensor.matmul_mx(
+                        out=results[h][:, first + j, :],
+                        lhsT=v_codes[:, cols].bitcast(FP8X4),
+                        lhsT_scale=v_scales[:, cols],
+                        rhs=weight_codes[h][:].bitcast(FP8X4),
+                        rhs_scale=weight_scales[h][:],
+                        start=True,
+                        stop=True,
+                    )
+
+        def store_pair(first, queue, rows, copy):
+            for h in reversed(range(HALVES)):
+                copy(out=rows[:, :, halves[h]], in_=results[h][:, first : first + 2, :])
+            queue.dma_start(out=out_rows[:, first : first + 2, :], in_=rows[:])
+
+        def codes_tile(t):
+            return sb.tile([P, P], U32, name="value_codes_%d" % t, align_bytes=64)
+
+        multiply(0, 1, turn(0, [picked_0], "values_turned_0", nc.scalar.copy), codes_tile(0))
+        multiply(1, 1, turn(1, [pick(1, "pool_0")], "gates_turned_0", nc.vector.tensor_copy), codes_tile(1))
+        picked_2 = pick_on_scalar(2, pieces=2)
+        picked = pick(3, "picked_3")
+        store_pair(0, nc.sync, lane.tile([P, 2, Q], F32, name="out_rows_0", offset=0, align_bytes=64), nc.vector.tensor_copy)
+        values_bf_2 = turn(2, [picked_2], "shares_turned", nc.scalar.copy)
+        values_bf_3 = turn(3, [picked], "values_turned_0", nc.scalar.copy)
+        multiply(2, 1, values_bf_2, lane.tile([P, P], U32, name="value_codes_2", offset=4096, align_bytes=64))
+        multiply(3, 1, values_bf_3, codes_tile(3))
 
         out_bf = [sb.tile([P, P, PACK], BF16, name="out_bf_%d" % h, align_bytes=64) for h in range(HALVES)]
         nc.vector.tensor_copy(out=out_bf[0][:], in_=results[0][:].rearrange("p t q -> p q t"))
@@ -249,7 +299,7 @@ def tile_attend_pagetimessigmoid_pl_kernel(tc, query, keys_words, keys_scales, t
                 scales=out_scales[:, halves[h]],
                 in_=out_bf[h][:].rearrange("p q t -> p (q t)"),
             )
-        nc.scalar.dma_start(out=out_planes[PACK - 1], in_=store_plane(PACK - 1)[:])
+        store_pair(2, nc.scalar, sb.tile([P, 2, Q], F32, name="out_rows_2"), nc.scalar.copy)
         nc.sync.dma_start(out=out_1[0].rearrange("p c r -> p (c r)").bitcast(I32), in_=out_codes[:].bitcast(I32))
         for quad in range(4):
             queue = nc.sync if quad < 2 else nc.scalar

from contextlib import ExitStack

import concourse.mybir as mybir
from concourse.masks import make_identity

D, E, T, I, Q, G = 512, 512, 2048, 512, 256, 32
FLOPS = 2 * D * I * Q + 2 * I * E * Q

F32 = mybir.dt.float32
BF16 = mybir.dt.bfloat16
I32 = mybir.dt.int32
U32 = mybir.dt.uint32
U16 = mybir.dt.uint16
U8 = mybir.dt.uint8
FP8X4 = mybir.dt.float8_e4m3fn_x4
FP4X4 = mybir.dt.float4_e2m1fn_x4
ACT = mybir.ActivationFunctionType
ALU = mybir.AluOpType
AXIS = mybir.AxisListType

P = 128
PACK = 4
HALVES = Q // P
PAGE = I // G
RUN = 4


def tile_attend_pagetimessigmoid_pl_kernel(tc, query, keys_words, keys_scales, th, sharp, slot_factor, vals, offs, out_0, out_1, out_2):
    nc = tc.nc
    with ExitStack() as ctx:
        sb = ctx.enter_context(tc.tile_pool(name="sb", bufs=1))
        lane = ctx.enter_context(tc.tile_pool(name="lane", bufs=1))
        ps = ctx.enter_context(tc.psum_pool(name="ps", bufs=1))

        offsets = sb.tile([P, I // 16], U16, name="offsets")
        nc.sync.dma_start(offsets[:], offs)

        key_word_pool = sb.tile([P, T], U16, name="key_word_pool", tag="pool_2", align_bytes=64)
        nc.sync.dma_start(out=key_word_pool[:].bitcast(I32), in_=keys_words[0].bitcast(I32))
        query_rows = sb.tile([P, PACK, Q], F32, name="query_rows")
        nc.sync.dma_start(out=query_rows[:], in_=query.rearrange("(p t) q -> p t q", t=PACK))

        warm_in = sb.tile([P, 1], F32, name="warm_in", tag="pool_0", align_bytes=64)
        warm_out = sb.tile([P, 1], F32, name="warm_out", tag="pool_1", align_bytes=64)
        nc.vector.memset(warm_in[:], 0.0)
        nc.scalar.activation(out=warm_out[:], in_=warm_in[:], func=ACT.Sigmoid)

        key_scale_pool = lane.tile([P, T], U8, name="key_scale_pool", offset=0, align_bytes=64)
        nc.vector.memset(key_scale_pool[:].bitcast(I32), 0)
        for quad in range(4):
            nc.sync.dma_start(
                out=key_scale_pool[32 * quad : 32 * quad + 4, :].bitcast(I32),
                in_=keys_scales[0, 4 * quad : 4 * quad + 4, :].bitcast(I32),
            )

        row_terms = sb.tile([P, P], F32, name="row_terms")
        nc.gpsimd.memset(row_terms[:], 0.0)
        nc.gpsimd.dma_start(out=row_terms[HALVES : 2 * HALVES, :], in_=sharp.rearrange("(h p) o -> h (p o)", p=P))
        nc.gpsimd.dma_start(out=row_terms[0:HALVES, :], in_=th.rearrange("(h p) o -> h (p o)", p=P))
        identity = sb.tile([P, P], F32, name="identity")
        make_identity(nc, identity[:])
        os_cols = sb.tile([P, PACK], F32, name="os_cols")
        nc.gpsimd.dma_start(out=os_cols[:], in_=slot_factor.rearrange("o (s r) -> (o s) r", r=PACK))

        value_planes = vals.rearrange("(p t) n -> t p n", t=PACK)
        value_pools = []

        def load_values(t, pieces=1):
            if t == PACK - 1:
                pool_t = lane.tile([P, T], F32, name="value_pool_%d" % t, offset=0, align_bytes=64)
            else:
                pool_t = sb.tile([P, T], F32, name="value_pool_%d" % t, tag="pool_%d" % t, align_bytes=64)
            for j in range(pieces):
                cols = slice(j * T // pieces, (j + 1) * T // pieces)
                nc.sync.dma_start(out=pool_t[:, cols], in_=value_planes[t][:, cols])
            value_pools.append(pool_t)

        load_values(0)
        load_values(1)

        terms_turned = ps.tile([P, P], F32, name="terms_turned", tag="half_0")
        nc.tensor.transpose(terms_turned[:], row_terms[:], identity[:])
        minus_th = sb.tile([P, HALVES], F32, name="minus_th")
        nc.scalar.activation(out=minus_th[:], in_=terms_turned[:, 0:HALVES], func=ACT.Copy, scale=-1.0)
        minus_sharp = sb.tile([P, HALVES], F32, name="minus_sharp")
        nc.scalar.activation(
            out=minus_sharp[:], in_=terms_turned[:, HALVES : 2 * HALVES], func=ACT.Copy, scale=-1.0 / PAGE
        )

        key_words = sb.tile([P, I], U16, name="key_words", align_bytes=64)
        nc.vector.tensor_copy(key_words[:], key_word_pool[:].indirect(offsets[:]))
        key_scales = sb.tile([P, I], U8, name="key_scales", align_bytes=64)
        nc.vector.tensor_copy(key_scales[:], key_scale_pool[:].indirect(offsets[:]))

        query_bf = sb.tile([P, Q, PACK], BF16, name="query_bf", align_bytes=64)
        nc.scalar.copy(
            out=query_bf[:].rearrange("p (c i) t -> p c t i", i=RUN),
            in_=query_rows[:].rearrange("p t (c i) -> p c t i", i=RUN),
        )
        query_codes = lane.tile([P, Q], U32, name="query_codes", offset=0, align_bytes=64)
        query_scales = sb.tile([P, Q], U8, name="query_scales", align_bytes=64)
        nc.vector.quantize_mx(
            out=query_codes[:].bitcast(FP8X4), scales=query_scales[:], in_=query_bf[:].rearrange("p q t -> p (q t)")
        )

        load_values(2, pieces=2)

        halves = [slice(h * P, (h + 1) * P) for h in range(HALVES)]
        scores = []
        for h in range(HALVES):
            bank = ps.tile([P, I], F32, name="scores_%d" % h, tag="half_%d" % h)
            nc.tensor.matmul_mx(
                out=bank[:],
                lhsT=query_codes[:, halves[h]].bitcast(FP8X4),
                lhsT_scale=query_scales[:, halves[h]],
                rhs=key_words[:].bitcast(FP4X4),
                rhs_scale=key_scales[:],
                start=True,
                stop=True,
            )
            scores.append(bank)

        load_values(3)

        picked_0 = sb.tile([P, I], BF16, name="picked_0", align_bytes=64)
        nc.vector.tensor_copy(picked_0[:], value_pools[0][:].indirect(offsets[:]))

        page_sums = sb.tile([P, HALVES, G], F32, name="page_sums", tag="pool_0", align_bytes=64)
        minus_s = sb.tile([P, HALVES, G], F32, name="minus_s", tag="gated", align_bytes=64)
        minus_top = sb.tile([P, HALVES], F32, name="minus_top")
        gates = []
        for h in range(HALVES):
            gate = sb.tile([P, PACK, P], F32, name="gate_%d" % h)
            nc.scalar.activation(
                out=gate[:],
                in_=scores[h][:].rearrange("p (s r) -> p r s", r=PACK),
                func=ACT.Sigmoid,
                bias=minus_th[:, h : h + 1],
            )
            gates.append(gate)
        for h in range(HALVES):
            nc.vector.tensor_reduce(
                out=page_sums[:, h, :], in_=scores[h][:].rearrange("p (g j) -> p g j", j=PAGE), axis=AXIS.X, op=ALU.add
            )
        for h in range(HALVES):
            nc.vector.tensor_scalar(
                out=minus_s[:, h, :],
                in0=page_sums[:, h, :],
                scalar1=minus_sharp[:, h : h + 1],
                scalar2=None,
                op0=ALU.mult,
                op1=ALU.min,
                accum_out=minus_top[:, h : h + 1],
            )
        sig = sb.tile([P, HALVES, G], F32, name="sig")
        for h in range(HALVES):
            nc.scalar.activation(
                out=sig[:, h, :], in_=minus_s[:, h, :], func=ACT.Sigmoid, scale=-1.0, bias=minus_top[:, h : h + 1]
            )
        rest = sb.tile([P, HALVES, G], F32, name="rest")
        nc.scalar.activation(out=rest[:], in_=sig[:], func=ACT.Copy, scale=-1.0, bias=1.0)
        rest_inv = sb.tile([P, HALVES, G], F32, name="rest_inv")
        nc.vector.reciprocal(out=rest_inv[:], in_=rest[:])
        page_exp = sb.tile([P, HALVES, G], F32, name="page_exp", tag="pool_bf", align_bytes=64)
        row_sum = sb.tile([P, HALVES], F32, name="row_sum", tag="values_bf_1", align_bytes=64)
        for h in range(HALVES):
            nc.vector.scalar_tensor_tensor(
                out=page_exp[:, h, :],
                in0=sig[:, h, :],
                scalar=1.0,
                in1=rest_inv[:, h, :],
                op0=ALU.mult,
                op1=ALU.mult,
                accum_out=row_sum[:, h : h + 1],
            )
        row_inv = sb.tile([P, HALVES], F32, name="row_inv")
        nc.vector.reciprocal(out=row_inv[:], in_=row_sum[:])
        shares = sb.tile([P, HALVES, P], F32, name="shares")
        shares_turned = ps.tile([P, Q], F32, name="shares_turned", tag="shares_turned")
        for h in range(HALVES):
            nc.scalar.activation(
                out=shares[:, h, :].rearrange("p (g j) -> p g j", j=P // G),
                in_=page_exp[:, h, :].rearrange("p (g o) -> p g o", o=1).to_broadcast([P, G, P // G]),
                func=ACT.Copy,
                scale=row_inv[:, h : h + 1],
            )
            nc.tensor.transpose(shares_turned[:, halves[h]], shares[:, h, :], identity[:])

        gated = sb.tile([P, Q // RUN, PACK, RUN], F32, name="gated", tag="gated", align_bytes=64)
        for pair in range(PACK // 2):
            turned = ps.tile([P, 2, Q], F32, name="gates_turned_%d" % pair, tag="gates_turned_%d" % pair)
            for h in range(HALVES):
                for e in range(2):
                    nc.tensor.transpose(turned[:, e, halves[h]], gates[h][:, 2 * pair + e, :], identity[:])
            for e in range(2):
                r = 2 * pair + e
                nc.scalar.activation(
                    out=gated[:, :, r, :],
                    in_=turned[:, e, :].rearrange("p (c i) -> p c i", i=RUN),
                    func=ACT.Copy,
                    scale=os_cols[:, r : r + 1],
                )

        weight_codes, weight_scales = [], []
        weights_bf = []
        for h in range(HALVES):
            w_bf = sb.tile([P, P, PACK], BF16, name="weights_bf_%d" % h, tag="weights_bf_%d" % h, align_bytes=64)
            nc.vector.tensor_tensor(
                out=w_bf[:].rearrange("p (c i) r -> p c r i", i=RUN),
                in0=gated[:, h * P // RUN : (h + 1) * P // RUN, :, :],
                in1=shares_turned[:, halves[h]]
                .rearrange("p (c o i) -> p c o i", o=1, i=RUN)
                .to_broadcast([P, P // RUN, PACK, RUN]),
                op=ALU.mult,
            )
            weights_bf.append(w_bf)
        for h in range(HALVES):
            codes = sb.tile([P, P], U32, name="weight_codes_%d" % h, align_bytes=64)
            scales = sb.tile([P, P], U8, name="weight_scales_%d" % h, align_bytes=64)
            nc.vector.quantize_mx(
                out=codes[:].bitcast(FP8X4), scales=scales[:], in_=weights_bf[h][:].rearrange("p q r -> p (q r)")
            )
            weight_codes.append(codes)
            weight_scales.append(scales)

        results = [ps.tile([P, PACK, P], F32, name="result_%d" % h, tag="half_%d" % h) for h in range(HALVES)]
        out_rows = out_0.rearrange("(p t) q -> p t q", t=PACK)

        def pick(t, tag):
            picked = sb.tile([P, I], BF16, name="picked_%d" % t, tag=tag, align_bytes=64)
            nc.vector.tensor_copy(picked[:], value_pools[t][:].indirect(offsets[:]))
            return picked

        def pick_on_scalar(t, pieces):
            pool_bf = sb.tile([P, T], BF16, name="value_pool_bf", tag="pool_bf", align_bytes=64)
            for j in range(pieces):
                cols = slice(j * T // pieces, (j + 1) * T // pieces)
                nc.scalar.activation(out=pool_bf[:, cols], in_=value_pools[t][:, cols], func=ACT.Copy)
            picked = sb.tile([P, I], BF16, name="picked_%d" % t, tag="weights_bf_0", align_bytes=64)
            nc.scalar.activation(out=picked[:], in_=pool_bf[:].indirect(offsets[:]), func=ACT.Copy)
            return picked

        def turn(first, picks, bank_tag, copy):
            n = len(picks)
            turned = ps.tile([P, n, 2, P], F32, name="values_turned_%d" % first, tag=bank_tag)
            for j in range(n):
                pairs = picks[j][:].bitcast(F32)
                for u in range(2):
                    nc.tensor.transpose(turned[:, j, u, :], pairs[:, u::2], identity[:])
            v_bf = sb.tile([P, n * P * PACK], BF16, name="values_bf_%d" % first, tag="values_bf_%d" % first, align_bytes=64)
            copy(
                out=v_bf[:].bitcast(F32).rearrange("p (j e u) -> p j e u", j=n, u=2),
                in_=turned[:].rearrange("p j u e -> p j e u"),
            )
            return v_bf

        def multiply(first, n, v_bf, v_codes):
            v_scales = sb.tile([P, n * P], U8, name="value_scales_%d" % first, align_bytes=64)
            nc.vector.quantize_mx(out=v_codes[:].bitcast(FP8X4), scales=v_scales[:], in_=v_bf[:])
            for j in range(n):
                cols = slice(j * P, (j + 1) * P)
                for h in range(HALVES):
                    nc.tensor.matmul_mx(
                        out=results[h][:, first + j, :],
                        lhsT=v_codes[:, cols].bitcast(FP8X4),
                        lhsT_scale=v_scales[:, cols],
                        rhs=weight_codes[h][:].bitcast(FP8X4),
                        rhs_scale=weight_scales[h][:],
                        start=True,
                        stop=True,
                    )

        def store_pair(first, queue, rows, copy):
            for h in reversed(range(HALVES)):
                copy(out=rows[:, :, halves[h]], in_=results[h][:, first : first + 2, :])
            queue.dma_start(out=out_rows[:, first : first + 2, :], in_=rows[:])

        def codes_tile(t):
            return sb.tile([P, P], U32, name="value_codes_%d" % t, align_bytes=64)

        multiply(0, 1, turn(0, [picked_0], "values_turned_0", nc.scalar.copy), codes_tile(0))
        multiply(1, 1, turn(1, [pick(1, "pool_0")], "gates_turned_0", nc.vector.tensor_copy), codes_tile(1))
        picked_2 = pick_on_scalar(2, pieces=2)
        picked = pick(3, "picked_3")
        store_pair(0, nc.sync, lane.tile([P, 2, Q], F32, name="out_rows_0", offset=0, align_bytes=64), nc.vector.tensor_copy)
        values_bf_2 = turn(2, [picked_2], "shares_turned", nc.scalar.copy)
        values_bf_3 = turn(3, [picked], "values_turned_0", nc.scalar.copy)
        multiply(2, 1, values_bf_2, lane.tile([P, P], U32, name="value_codes_2", offset=4096, align_bytes=64))
        multiply(3, 1, values_bf_3, codes_tile(3))

        out_bf = [sb.tile([P, P, PACK], BF16, name="out_bf_%d" % h, align_bytes=64) for h in range(HALVES)]
        nc.vector.tensor_copy(out=out_bf[0][:], in_=results[0][:].rearrange("p t q -> p q t"))
        nc.scalar.copy(out=out_bf[1][:], in_=results[1][:].rearrange("p t q -> p q t"))
        out_codes = sb.tile([P, Q], U32, name="out_codes", align_bytes=64)
        out_scales = sb.tile([P, Q], U8, name="out_scales", align_bytes=64)
        for h in range(HALVES):
            nc.vector.quantize_mx(
                out=out_codes[:, halves[h]].bitcast(FP8X4),
                scales=out_scales[:, halves[h]],
                in_=out_bf[h][:].rearrange("p q t -> p (q t)"),
            )
        store_pair(2, nc.scalar, sb.tile([P, 2, Q], F32, name="out_rows_2"), nc.scalar.copy)
        nc.sync.dma_start(out=out_1[0].rearrange("p c r -> p (c r)").bitcast(I32), in_=out_codes[:].bitcast(I32))
        for quad in range(4):
            queue = nc.sync if quad < 2 else nc.scalar
            queue.dma_start(
                out=out_2[0, 4 * quad : 4 * quad + 4, :].bitcast(I32),
                in_=out_scales[32 * quad : 32 * quad + 4, :].bitcast(I32),
            )
